import numpy as np
import ml_dtypes


def mxq(x, axis, fmt="e4m3"):
    dtype, down = {"e4m3": (ml_dtypes.float8_e4m3fn, 7), "e5m2": (ml_dtypes.float8_e5m2, 14)}[fmt]
    v = np.moveaxis(np.asarray(x, np.float32).astype(ml_dtypes.bfloat16).astype(np.float64), axis, -1)
    blocks = v.reshape(v.shape[:-1] + (-1, 32))
    amax = np.abs(blocks).max(-1, keepdims=True)
    byte = np.maximum(np.where(amax > 0, np.frexp(amax)[1] - 1 + 127, 0) - down, 1)
    scale = np.exp2(byte - 127.0)
    codes = (blocks / scale).astype(np.float32).astype(dtype).astype(np.float64)
    return np.moveaxis((codes * scale).reshape(v.shape), -1, axis)


WIDE = False


def mx_kscale(k):
    if not WIDE:
        return np.ones(k)
    levels = np.array([30, -30])
    if k % 512:
        return np.exp2(np.random.permutation(np.resize(levels, k // 32))).repeat(32)
    a = np.empty((k // 512, 16))
    for p in range(k // 512):
        a[p, :8] = np.random.permutation(np.resize(levels, 8))
        for g in range(8):
            far = levels[np.abs(levels - a[p, g]) >= 10]
            a[p, g + 8] = far[np.random.randint(len(far))]
    return np.exp2(a.ravel()).repeat(32)


def f64(x):
    return np.asarray(x).astype(np.float64)


def striped(idx):
    return np.tile(idx.reshape(-1, 16).T, (8, 1)).astype(np.uint16)


def unstriped(offs):
    return offs[:16].T.reshape(-1).astype(np.int64)


E2M1 = np.array([0.0, 0.5, 1.0, 1.5, 2.0, 3.0, 4.0, 6.0, -0.0, -0.5, -1.0, -1.5, -2.0, -3.0, -4.0, -6.0])


def pack_weight(w, fmt):
    k, n = w.shape
    w = f64(np.asarray(w, np.float32).astype(ml_dtypes.bfloat16)).reshape(k // 32, 32, n)
    amax = np.abs(w).max(1)
    if fmt == "e4m3":
        byte = np.frexp(amax)[1] - 1 + 127 - 7
    else:
        mant, ex = np.frexp(amax / 6.0)
        byte = np.where(mant > 0.5, ex, ex - 1) + 127
    byte = np.clip(np.where(amax > 0, byte, 1), 1, 254)
    scaled = (w * np.exp2(127.0 - byte)[:, None, :]).reshape(k, n).astype(np.float32)
    by_word = np.ascontiguousarray(scaled.reshape(k // 512, 128, 4, n).transpose(0, 1, 3, 2))
    if fmt == "e4m3":
        words = by_word.astype(ml_dtypes.float8_e4m3fn).view(np.uint8)
    else:
        c = by_word.astype(ml_dtypes.float4_e2m1fn).view(np.uint8) & 0xF
        words = (c[..., 0::2] | (c[..., 1::2] << 4)).reshape(k // 512, 128, 2 * n)
    return np.ascontiguousarray(words), np.ascontiguousarray(byte.astype(np.uint8).reshape(k // 512, 16, n))


def unpack_weight(words, scales, fmt):
    g, _, n = scales.shape
    words = np.ascontiguousarray(words).reshape(g, 128, n, -1)
    if fmt == "e4m3":
        vals = words.view(ml_dtypes.float8_e4m3fn).astype(np.float64)
    else:
        nib = np.empty((g, 128, n, 4), np.uint8)
        nib[..., 0::2] = words & 0xF
        nib[..., 1::2] = words >> 4
        vals = E2M1[nib]
    vals = vals * np.repeat(np.exp2(scales.astype(np.float64) - 127.0), 8, axis=1)[..., None]
    return vals.transpose(0, 1, 3, 2).reshape(g * 512, n)


K, T, E, C, N = 128, 1536, 2, 512, 1536


def by_expert(wq, xq):
    return np.concatenate([wq[e].T @ xq[:, e * C:(e + 1) * C] for e in range(E)], axis=1)


def setup_inputs():
    n = np.random.standard_normal
    s = mx_kscale(N)[:, None]
    w = [pack_weight(m, "e2m1") for m in n((E + 1, N, K)) / np.sqrt(N) / s[None]]
    return {
        "dyT": (n((N, T)) * s).astype(np.float32),
        "w_words": np.stack([m[0] for m in w]),
        "w_scales": np.stack([m[1] for m in w]),
        "gate": np.tile(np.random.uniform(0.2, 1.0, E * C), (N, 1)).astype(np.float32),
        "offs": striped(np.random.permutation(T)[:E * C]),
    }


def reference(dyT, w_words, w_scales, gate, offs):
    idx = unstriped(offs)
    w = np.stack([unpack_weight(w_words[e], w_scales[e], "e2m1") for e in range(E + 1)])
    gq = mxq(f64(gate) * f64(dyT)[:, idx], 0, "e5m2")
    wq = w
    ds = wq[E].T @ mxq(f64(dyT), 0, "e5m2")
    dx = by_expert(wq, gq)
    ds[:, idx] += dx
    return ds

@@ -1,0 +1,282 @@
+from contextlib import ExitStack
+
+import concourse.mybir as mybir
+from concourse.masks import make_identity
+
+K, T, E, C, N = 128, 1536, 2, 512, 1536
+S = E * C
+P = 128
+PACK = 4
+K_PASS = P * PACK
+PASSES = N // K_PASS
+COLS = 512
+CHUNKS = T // COLS
+BLOCKS = S // P
+
+F32 = mybir.dt.float32
+BF16 = mybir.dt.bfloat16
+I32 = mybir.dt.int32
+U32 = mybir.dt.uint32
+U16 = mybir.dt.uint16
+U8 = mybir.dt.uint8
+E5M2X4 = mybir.dt.float8_e5m2_x4
+E2M1X4 = mybir.dt.float4_e2m1fn_x4
+MULT = mybir.AluOpType.mult
+ADD = mybir.AluOpType.add
+COPY = mybir.ActivationFunctionType.Copy
+
+FLOPS = 2 * N * K * (S + T)
+BYTES = 4 * N * T + 3 * N * K // 2 + 3 * N * K // 32 + 4 * S + 2 * 128 * 64 + 4 * K * T
+
+MODES = "PDD"
+
+
+def tile_moe_bds_lin_none_kernel(tc, dyT, w_words, w_scales, gate, offs, out):
+    nc = tc.nc
+    with ExitStack() as ctx:
+        keep = ctx.enter_context(tc.tile_pool(name="keep", bufs=1))
+        ring = ctx.enter_context(tc.tile_pool(name="ring", bufs=2))
+        reuse = ctx.enter_context(tc.tile_pool(name="reuse", bufs=1))
+        front = ctx.enter_context(tc.tile_pool(name="front", bufs=1))
+        psum = ctx.enter_context(tc.psum_pool(name="psum", bufs=1))
+
+        offsets = keep.tile([P, S // 16], U16, name="offsets")
+        nc.sync.dma_start(offsets[:], offs)
+
+        rows = [dyT[a * K_PASS : (a + 1) * K_PASS, :].rearrange("(p j) t -> p j t", j=PACK) for a in range(PASSES)]
+
+        w_codes = keep.tile([P, (E + 1) * PASSES, 2 * K], U8, name="w_codes", align_bytes=64)
+        w_plane = keep.tile([P, (E + 1) * PASSES, K], U8, name="w_plane", align_bytes=64)
+        routed_out = keep.tile([P, T], F32, name="routed_out")
+        ident = keep.tile([P, P], F32, name="ident")
+        gate_rows = keep.tile([P, P], F32, name="gate_rows")
+        gate_cols = keep.tile([P, BLOCKS], F32, name="gate_cols")
+        gate_all = keep.tile([P, S], F32, name="gate_all")
+
+        nc.vector.memset(w_plane[:].rearrange("p m k -> p (m k)").bitcast(I32), 0)
+        nc.vector.memset(routed_out[:], 0.0)
+        if "P" in MODES:
+            make_identity(nc, ident[:])
+        scale_rows = w_scales.rearrange("e a (q r) k -> r q (e a) k", r=4)
+
+        def load_scales():
+            for r in range(4):
+                nc.sync.dma_start(w_plane[r:P:32].bitcast(I32), scale_rows[r].bitcast(I32))
+
+        def load_gate_rows():
+            nc.sync.dma_start(gate_rows[:], gate[0:16, :].rearrange("r (b s) -> (r b) s", s=P))
+
+        whole = {}
+        window = {}
+        dense = {}
+
+        def load_planes(a, d0, d1, lo, hi):
+            if a not in whole:
+                whole[a] = front.tile([P, PACK, T], F32, name="whole", offset=0)
+            nc.sync.dma_start(whole[a][:, d0:d1, lo:hi], rows[a][:, d0:d1, lo:hi])
+
+        def load_window(a, d):
+            window[a, d] = ring.tile([P, T], F32, name="window", bufs=8)
+            nc.sync.dma_start(window[a, d][:], rows[a][:, d, :])
+
+        def load_dense(a, c):
+            if a == 2:
+                dense[a, c] = front.tile([P, PACK, COLS], F32, name="late%d" % c, offset=c * PACK * COLS * 4)
+            else:
+                dense[a, c] = ring.tile([P, PACK, COLS], F32, name="dense", bufs=3)
+            nc.sync.dma_start(dense[a, c][:], rows[a][:, :, c * COLS : (c + 1) * COLS])
+
+        def load_gate(lo, hi):
+            nc.sync.dma_start(gate_all[:, lo:hi], gate[0:P, lo:hi])
+
+        def load_weights():
+            nc.sync.dma_start(w_codes[:].bitcast(I32), w_words.rearrange("e a p b -> p (e a) b").bitcast(I32))
+
+        load_gate_rows()
+        load_planes(0, 0, 1, 0, 1536)
+        load_planes(0, 1, 4, 0, 512)
+        load_planes(0, 1, 2, 512, 1536)
+        load_planes(0, 2, 3, 512, 1536)
+        load_planes(0, 3, 4, 512, 1536)
+        load_gate(0, 1024)
+        load_window(1, 2)
+        load_window(1, 0)
+        load_dense(1, 0)
+        load_window(2, 0)
+        load_window(1, 1)
+        load_window(1, 3)
+        load_window(2, 2)
+        load_window(2, 3)
+        load_window(2, 1)
+        load_weights()
+        load_scales()
+        load_dense(1, 2)
+        load_dense(1, 1)
+        load_dense(2, 2)
+        load_dense(2, 1)
+        load_dense(2, 0)
+
+        acc_s = [psum.tile([P, COLS], F32, name="acc_s%d" % c) for c in range(CHUNKS)]
+        acc_r = {}
+
+        if "P" in MODES:
+            gate_t = psum.tile([P, PACK, P], F32, name="turned", bufs=3)
+            nc.tensor.transpose(gate_t[:, 0, :], gate_rows[:], ident[:])
+            nc.scalar.activation(gate_cols[:], gate_t[:, 0, 0:BLOCKS], COPY)
+
+        stage = reuse.tile([P, PACK * S + BLOCKS * 2 * P], F32, name="stage", offset=0)
+        picked = {0: stage[:, 0 : PACK * S].rearrange("p (d s) -> p d s", d=PACK)}
+        gated_all = stage[:, PACK * S :].rearrange("p (b u w) -> p b u w", b=BLOCKS, u=2)
+        grouped_r = {}
+        grouped_s = {}
+
+        def interleave(dst, src):
+            nc.scalar.copy(
+                dst.rearrange("p (c i) t -> p c t i", i=4),
+                src.rearrange("p t (c i) -> p c t i", i=4),
+            )
+
+        def gather(a, d, lo, hi):
+            if a not in picked:
+                picked[a] = ring.tile([P, PACK, S], F32, name="picked", bufs=2)
+            lst = offsets[:, lo // 16 : hi // 16]
+            if MODES[a] == "P":
+                nc.vector.tensor_copy(picked[a][:, d, lo:hi], whole[a][:, d, :].indirect(lst))
+            else:
+                nc.vector.tensor_tensor(picked[a][:, d, lo:hi], window[a, d][:].indirect(lst), gate_all[:, lo:hi], MULT)
+
+        def round_routed(a, lo, hi):
+            if a not in grouped_r:
+                if a == 0:
+                    grouped_r[a] = keep.tile([P, S, PACK], BF16, name="grouped_r0", align_bytes=64)
+                else:
+                    grouped_r[a] = reuse.tile([P, S, PACK], BF16, name="grouped_r%d" % a, align_bytes=64, offset=13824 + (a - 1) * 8192)
+            if MODES[a] == "D":
+                for x in range(lo, hi, COLS):
+                    interleave(grouped_r[a][:, x : x + COLS, :], picked[a][:, :, x : x + COLS])
+                return
+            words = grouped_r[a][:].rearrange("p s t -> p (s t)").bitcast(F32)
+            for pair in range(lo // (2 * P), hi // (2 * P)):
+                back = psum.tile([P, 2, 2, P], F32, name="back", bufs=2)
+                for h in range(2):
+                    b = 2 * pair + h
+                    turned = psum.tile([P, PACK, P], F32, name="turned", bufs=3)
+                    for d in range(PACK):
+                        nc.tensor.transpose(turned[:, d, :], picked[a][:, d, b * P : (b + 1) * P], ident[:])
+                    gated = gated_all[:, b, :, :]
+                    nc.scalar.activation(
+                        gated.bitcast(BF16).rearrange("s u (p e) -> s u p e", e=2),
+                        turned[:].rearrange("s (u e) p -> s u p e", e=2),
+                        COPY,
+                        scale=gate_cols[:, b : b + 1],
+                    )
+                    for u in range(2):
+                        nc.tensor.transpose(back[:, h, u, :], gated[:, u, :], ident[:])
+                nc.scalar.copy(
+                    words[:, pair * 4 * P : (pair + 1) * 4 * P].rearrange("p (h s u) -> p h s u", h=2, u=2),
+                    back[:].rearrange("p h u s -> p h s u"),
+                )
+
+        def round_shared(a, c):
+            if a == 1:
+                grouped_s[a, c] = reuse.tile([P, COLS, PACK], BF16, name="grouped_s1%d" % c, align_bytes=64, offset=c * 4096)
+            else:
+                grouped_s[a, c] = ring.tile([P, COLS, PACK], BF16, name="grouped_s", bufs=3, align_bytes=64)
+            src = whole[a][:, :, c * COLS : (c + 1) * COLS] if MODES[a] == "P" else dense[a, c][:]
+            interleave(grouped_s[a, c][:], src)
+
+        def multiply(acc, e, a, codes, plane):
+            m = e * PASSES + a
+            nc.tensor.matmul_mx(
+                acc[:],
+                lhsT=w_codes[:, m, :].bitcast(E2M1X4),
+                lhsT_scale=w_plane[:, m, :],
+                rhs=codes.bitcast(E5M2X4),
+                rhs_scale=plane,
+                start=(a == 0),
+                stop=(a == PASSES - 1),
+            )
+
+        def quantise_routed(a, lo, hi):
+            codes = ring.tile([P, hi - lo], U32, name="codes_r", bufs=2, align_bytes=64)
+            plane = ring.tile([P, hi - lo], U8, name="plane_r", bufs=2, align_bytes=64)
+            nc.vector.quantize_mx(codes[:].bitcast(E5M2X4), plane[:], grouped_r[a][:, lo:hi, :].rearrange("p s t -> p (s t)"))
+            for x in range(lo, hi, C):
+                if a == 0:
+                    acc_r[x // C] = psum.tile([P, COLS], F32, name="acc_r", tag="back", bufs=2)
+                multiply(acc_r[x // C], x // C, a, codes[:, x - lo : x - lo + C], plane[:, x - lo : x - lo + C])
+
+        def quantise_shared(a, c):
+            codes = ring.tile([P, COLS], U32, name="codes_s", bufs=5, align_bytes=64)
+            if a == 0:
+                plane = reuse.tile([P, COLS], U8, name="plane_first%d" % c, align_bytes=64, offset=12288 + c * COLS)
+            else:
+                plane = ring.tile([P, COLS], U8, name="plane_s", bufs=5, align_bytes=64)
+            nc.vector.quantize_mx(codes[:].bitcast(E5M2X4), plane[:], grouped_s[a, c][:].rearrange("p s t -> p (s t)"))
+            multiply(acc_s[c], E, a, codes[:], plane[:])
+
+        sums = {}
+
+        def fetch(e):
+            sums[e] = keep.tile([P, C], F32, name="sums%d" % e)
+            nc.scalar.copy(sums[e][:], acc_r[e][:])
+
+        def scatter(e):
+            nc.vector.tensor_copy(routed_out[:].indirect(offsets[:, e * C // 16 : (e + 1) * C // 16]), sums[e][:])
+
+        def finish(c):
+            cols = slice(c * COLS, (c + 1) * COLS)
+            total = keep.tile([P, COLS], F32, name="total%d" % c)
+            nc.vector.tensor_tensor(total[:], routed_out[:, cols], acc_s[c][:], ADD)
+            nc.sync.dma_start(out[:, cols], total[:])
+
+        gather(0, 0, 0, 1024)
+        gather(0, 1, 0, 1024)
+        round_shared(0, 0)
+        round_shared(0, 1)
+        gather(0, 2, 0, 1024)
+        gather(0, 3, 0, 1024)
+        gather(1, 0, 0, 1024)
+        gather(1, 2, 0, 1024)
+        round_shared(0, 2)
+        round_routed(0, 0, 1024)
+        gather(2, 0, 0, 512)
+        quantise_shared(0, 1)
+        round_shared(1, 0)
+        gather(1, 1, 0, 1024)
+        gather(1, 3, 0, 1024)
+        round_routed(1, 0, 512)
+        gather(2, 2, 512, 1024)
+        gather(2, 2, 0, 512)
+        gather(2, 3, 0, 512)
+        gather(2, 1, 0, 512)
+        round_routed(1, 512, 1024)
+        quantise_shared(0, 2)
+        round_routed(2, 0, 512)
+        gather(2, 3, 512, 1024)
+        gather(2, 0, 512, 1024)
+        gather(2, 1, 512, 1024)
+        round_shared(1, 2)
+        quantise_routed(0, 0, 1024)
+        quantise_routed(1, 0, 1024)
+        round_shared(1, 1)
+        quantise_routed(2, 0, 512)
+        quantise_shared(1, 1)
+        round_routed(2, 512, 1024)
+        fetch(0)
+        quantise_shared(1, 2)
+        quantise_shared(0, 0)
+        quantise_routed(2, 512, 1024)
+        scatter(0)
+        round_shared(2, 2)
+        round_shared(2, 1)
+        fetch(1)
+        quantise_shared(2, 1)
+        scatter(1)
+        quantise_shared(1, 0)
+        quantise_shared(2, 2)
+        round_shared(2, 0)
+        quantise_shared(2, 0)
+        finish(2)
+        finish(1)
+        finish(0)

@@ -6,12 +6,19 @@ from concourse.masks import make_identity
 K, T, E, C, N = 128, 1536, 2, 512, 1536
 S = E * C
 P = 128
-PACK = 4
-K_PASS = P * PACK
-PASSES = N // K_PASS
+ROWS = 4
+PASSES = N // (P * ROWS)
 COLS = 512
 CHUNKS = T // COLS
 BLOCKS = S // P
+PER_COL = 16
+AHEAD = 6
+SCALE_ROWS = 4
+
+SHARED_BYTES = COLS * ROWS * 2
+SCALES_AT = CHUNKS * SHARED_BYTES
+ROUTED_AT = SCALES_AT + CHUNKS * COLS
+ROUTED_BYTES = S * ROWS * 2
 
 F32 = mybir.dt.float32
 BF16 = mybir.dt.bfloat16
@@ -26,9 +33,7 @@ ADD = mybir.AluOpType.add
 COPY = mybir.ActivationFunctionType.Copy
 
 FLOPS = 2 * N * K * (S + T)
-BYTES = 4 * N * T + 3 * N * K // 2 + 3 * N * K // 32 + 4 * S + 2 * 128 * 64 + 4 * K * T
-
-MODES = "PDD"
+BYTES = 4 * N * T + (E + 1) * N * K // 2 + (E + 1) * N * K // 32 + 4 * S + 2 * P * S // PER_COL + 4 * K * T
 
 
 def tile_moe_bds_lin_none_kernel(tc, dyT, w_words, w_scales, gate, offs, out):
@@ -40,243 +45,223 @@ def tile_moe_bds_lin_none_kernel(tc, dyT, w_words, w_scales, gate, offs, out):
         front = ctx.enter_context(tc.tile_pool(name="front", bufs=1))
         psum = ctx.enter_context(tc.psum_pool(name="psum", bufs=1))
 
-        offsets = keep.tile([P, S // 16], U16, name="offsets")
+        offsets = keep.tile([P, S // PER_COL], U16, name="offsets")
         nc.sync.dma_start(offsets[:], offs)
 
-        rows = [dyT[a * K_PASS : (a + 1) * K_PASS, :].rearrange("(p j) t -> p j t", j=PACK) for a in range(PASSES)]
+        dy = [dyT[a * P * ROWS : (a + 1) * P * ROWS, :].rearrange("(p d) t -> p d t", d=ROWS) for a in range(PASSES)]
 
         w_codes = keep.tile([P, (E + 1) * PASSES, 2 * K], U8, name="w_codes", align_bytes=64)
-        w_plane = keep.tile([P, (E + 1) * PASSES, K], U8, name="w_plane", align_bytes=64)
-        routed_out = keep.tile([P, T], F32, name="routed_out")
+        w_bytes = keep.tile([P, (E + 1) * PASSES, K], U8, name="w_bytes", align_bytes=64)
+        result = keep.tile([P, T], F32, name="result")
         ident = keep.tile([P, P], F32, name="ident")
         gate_rows = keep.tile([P, P], F32, name="gate_rows")
         gate_cols = keep.tile([P, BLOCKS], F32, name="gate_cols")
         gate_all = keep.tile([P, S], F32, name="gate_all")
 
-        nc.vector.memset(w_plane[:].rearrange("p m k -> p (m k)").bitcast(I32), 0)
-        nc.vector.memset(routed_out[:], 0.0)
-        if "P" in MODES:
-            make_identity(nc, ident[:])
-        scale_rows = w_scales.rearrange("e a (q r) k -> r q (e a) k", r=4)
+        nc.vector.memset(w_bytes[:].rearrange("p m k -> p (m k)").bitcast(I32), 0)
+        nc.vector.memset(result[:], 0.0)
+        make_identity(nc, ident[:])
 
-        def load_scales():
-            for r in range(4):
-                nc.sync.dma_start(w_plane[r:P:32].bitcast(I32), scale_rows[r].bitcast(I32))
-
-        def load_gate_rows():
-            nc.sync.dma_start(gate_rows[:], gate[0:16, :].rearrange("r (b s) -> (r b) s", s=P))
-
-        whole = {}
+        first = front.tile([P, ROWS, T], F32, name="first", offset=0)
         window = {}
         dense = {}
 
-        def load_planes(a, d0, d1, lo, hi):
-            if a not in whole:
-                whole[a] = front.tile([P, PACK, T], F32, name="whole", offset=0)
-            nc.sync.dma_start(whole[a][:, d0:d1, lo:hi], rows[a][:, d0:d1, lo:hi])
+        def load_first(d):
+            nc.sync.dma_start(first[:, d : d + 1, :], dy[0][:, d : d + 1, :])
 
         def load_window(a, d):
-            window[a, d] = ring.tile([P, T], F32, name="window", bufs=8)
-            nc.sync.dma_start(window[a, d][:], rows[a][:, d, :])
+            window[a, d] = ring.tile([P, T], F32, name="window", bufs=(PASSES - 1) * ROWS)
+            nc.sync.dma_start(window[a, d][:], dy[a][:, d, :])
 
         def load_dense(a, c):
-            if a == 2:
-                dense[a, c] = front.tile([P, PACK, COLS], F32, name="late%d" % c, offset=c * PACK * COLS * 4)
+            if a == PASSES - 1:
+                dense[a, c] = front.tile([P, ROWS, COLS], F32, name="late%d" % c, offset=c * ROWS * COLS * 4)
             else:
-                dense[a, c] = ring.tile([P, PACK, COLS], F32, name="dense", bufs=3)
-            nc.sync.dma_start(dense[a, c][:], rows[a][:, :, c * COLS : (c + 1) * COLS])
+                dense[a, c] = ring.tile([P, ROWS, COLS], F32, name="dense", bufs=CHUNKS)
+            nc.sync.dma_start(dense[a, c][:], dy[a][:, :, c * COLS : (c + 1) * COLS])
 
-        def load_gate(lo, hi):
-            nc.sync.dma_start(gate_all[:, lo:hi], gate[0:P, lo:hi])
+        def load_gate_rows():
+            nc.sync.dma_start(gate_rows[:], gate[0 : P // BLOCKS, :].rearrange("r (b s) -> (r b) s", s=P))
 
-        def load_weights():
+        def load_gate_all():
+            nc.sync.dma_start(gate_all[:], gate[0:P, :])
+
+        def load_weight_words():
             nc.sync.dma_start(w_codes[:].bitcast(I32), w_words.rearrange("e a p b -> p (e a) b").bitcast(I32))
 
+        def load_weight_scales():
+            by_row = w_scales.rearrange("e a (q r) k -> r q (e a) k", r=SCALE_ROWS)
+            for r in range(SCALE_ROWS):
+                nc.sync.dma_start(w_bytes[r:P:32].bitcast(I32), by_row[r].bitcast(I32))
+
+        last = PASSES - 1
+        load_first(0)
         load_gate_rows()
-        load_planes(0, 0, 1, 0, 1536)
-        load_planes(0, 1, 4, 0, 512)
-        load_planes(0, 1, 2, 512, 1536)
-        load_planes(0, 2, 3, 512, 1536)
-        load_planes(0, 3, 4, 512, 1536)
-        load_gate(0, 1024)
-        load_window(1, 2)
-        load_window(1, 0)
-        load_dense(1, 0)
-        load_window(2, 0)
-        load_window(1, 1)
-        load_window(1, 3)
-        load_window(2, 2)
-        load_window(2, 3)
-        load_window(2, 1)
-        load_weights()
-        load_scales()
-        load_dense(1, 2)
-        load_dense(1, 1)
-        load_dense(2, 2)
-        load_dense(2, 1)
-        load_dense(2, 0)
+        for d in range(1, ROWS):
+            load_first(d)
+        load_gate_all()
+        for d in range(ROWS):
+            load_window(1, d)
+        load_weight_words()
+        load_window(last, 0)
+        load_weight_scales()
+        for d in range(1, ROWS - 1):
+            load_window(last, d)
+        for c in range(CHUNKS - 1):
+            load_dense(1, c)
+            load_dense(last, c)
+        load_window(last, ROWS - 1)
+        load_dense(1, CHUNKS - 1)
+        load_dense(last, CHUNKS - 1)
 
-        acc_s = [psum.tile([P, COLS], F32, name="acc_s%d" % c) for c in range(CHUNKS)]
-        acc_r = {}
+        gate_turned = psum.tile([P, ROWS, P], F32, name="turned", bufs=AHEAD)
+        nc.tensor.transpose(gate_turned[:, 0, :], gate_rows[:], ident[:])
+        nc.scalar.activation(gate_cols[:], gate_turned[:, 0, 0:BLOCKS], COPY)
 
-        if "P" in MODES:
-            gate_t = psum.tile([P, PACK, P], F32, name="turned", bufs=3)
-            nc.tensor.transpose(gate_t[:, 0, :], gate_rows[:], ident[:])
-            nc.scalar.activation(gate_cols[:], gate_t[:, 0, 0:BLOCKS], COPY)
+        stage = reuse.tile([P, ROWS * S + BLOCKS * 2 * P], F32, name="stage", offset=0)
+        picked = {(0, 0): stage[:, 0 : ROWS * S].rearrange("p (d s) -> p d s", d=ROWS)}
+        gated = stage[:, ROWS * S :].rearrange("p (b u w) -> p b u w", b=BLOCKS, u=2)
+        routed = {}
+        shared = {}
+        acc_routed = {}
+        acc_shared = {}
+        sums = {}
 
-        stage = reuse.tile([P, PACK * S + BLOCKS * 2 * P], F32, name="stage", offset=0)
-        picked = {0: stage[:, 0 : PACK * S].rearrange("p (d s) -> p d s", d=PACK)}
-        gated_all = stage[:, PACK * S :].rearrange("p (b u w) -> p b u w", b=BLOCKS, u=2)
-        grouped_r = {}
-        grouped_s = {}
-
-        def interleave(dst, src):
-            nc.scalar.copy(
-                dst.rearrange("p (c i) t -> p c t i", i=4),
-                src.rearrange("p t (c i) -> p c t i", i=4),
-            )
+        def interleave(copy, dst, src):
+            copy(dst.rearrange("p (c i) d -> p c d i", i=2), src.rearrange("p d (c i) -> p c d i", i=2))
 
         def gather(a, d, lo, hi):
-            if a not in picked:
-                picked[a] = ring.tile([P, PACK, S], F32, name="picked", bufs=2)
-            lst = offsets[:, lo // 16 : hi // 16]
-            if MODES[a] == "P":
-                nc.vector.tensor_copy(picked[a][:, d, lo:hi], whole[a][:, d, :].indirect(lst))
+            if (a, lo) not in picked:
+                picked[a, lo] = ring.tile([P, ROWS, hi - lo], F32, name="picked%d_%d" % (a, lo), bufs=1)
+            slots = offsets[:, lo // PER_COL : hi // PER_COL]
+            if a == 0:
+                nc.vector.tensor_copy(picked[a, lo][:, d, :], first[:, d, :].indirect(slots))
             else:
-                nc.vector.tensor_tensor(picked[a][:, d, lo:hi], window[a, d][:].indirect(lst), gate_all[:, lo:hi], MULT)
+                nc.vector.tensor_tensor(picked[a, lo][:, d, :], window[a, d][:].indirect(slots), gate_all[:, lo:hi], MULT)
 
-        def round_routed(a, lo, hi):
-            if a not in grouped_r:
-                if a == 0:
-                    grouped_r[a] = keep.tile([P, S, PACK], BF16, name="grouped_r0", align_bytes=64)
-                else:
-                    grouped_r[a] = reuse.tile([P, S, PACK], BF16, name="grouped_r%d" % a, align_bytes=64, offset=13824 + (a - 1) * 8192)
-            if MODES[a] == "D":
-                for x in range(lo, hi, COLS):
-                    interleave(grouped_r[a][:, x : x + COLS, :], picked[a][:, :, x : x + COLS])
-                return
-            words = grouped_r[a][:].rearrange("p s t -> p (s t)").bitcast(F32)
-            for pair in range(lo // (2 * P), hi // (2 * P)):
-                back = psum.tile([P, 2, 2, P], F32, name="back", bufs=2)
-                for h in range(2):
-                    b = 2 * pair + h
-                    turned = psum.tile([P, PACK, P], F32, name="turned", bufs=3)
-                    for d in range(PACK):
-                        nc.tensor.transpose(turned[:, d, :], picked[a][:, d, b * P : (b + 1) * P], ident[:])
-                    gated = gated_all[:, b, :, :]
-                    nc.scalar.activation(
-                        gated.bitcast(BF16).rearrange("s u (p e) -> s u p e", e=2),
-                        turned[:].rearrange("s (u e) p -> s u p e", e=2),
-                        COPY,
-                        scale=gate_cols[:, b : b + 1],
-                    )
-                    for u in range(2):
-                        nc.tensor.transpose(back[:, h, u, :], gated[:, u, :], ident[:])
-                nc.scalar.copy(
-                    words[:, pair * 4 * P : (pair + 1) * 4 * P].rearrange("p (h s u) -> p h s u", h=2, u=2),
-                    back[:].rearrange("p h u s -> p h s u"),
+        def gate_first_pass():
+            routed[0] = keep.tile([P, S, ROWS], BF16, name="routed0", align_bytes=64)
+            words = routed[0][:].rearrange("p s d -> p (s d)").bitcast(F32)
+            turned = {}
+            back = {}
+
+            def turn(b):
+                turned[b] = psum.tile([P, ROWS, P], F32, name="turned", bufs=AHEAD)
+                for d in range(ROWS):
+                    nc.tensor.transpose(turned[b][:, d, :], picked[0, 0][:, d, b * P : (b + 1) * P], ident[:])
+
+            for b in range(AHEAD):
+                turn(b)
+            for b in range(BLOCKS):
+                pair, h = divmod(b, 2)
+                nc.scalar.activation(
+                    gated[:, b, :, :].bitcast(BF16).rearrange("s u (p e) -> s u p e", e=2),
+                    turned[b][:].rearrange("s (u e) p -> s u p e", e=2),
+                    COPY,
+                    scale=gate_cols[:, b : b + 1],
                 )
+                if b + AHEAD < BLOCKS:
+                    turn(b + AHEAD)
+                if h == 0:
+                    back[pair] = psum.tile([P, 2, 2, P], F32, name="back", bufs=E)
+                for u in range(2):
+                    nc.tensor.transpose(back[pair][:, h, u, :], gated[:, b, u, :], ident[:])
+                if h == 1:
+                    nc.scalar.copy(
+                        words[:, pair * 4 * P : (pair + 1) * 4 * P].rearrange("p (h s u) -> p h s u", h=2, u=2),
+                        back[pair][:].rearrange("p h u s -> p h s u"),
+                    )
 
-        def round_shared(a, c):
+        def round_routed(a, e):
+            if a not in routed:
+                at = ROUTED_AT + (a - 1) * ROUTED_BYTES
+                routed[a] = reuse.tile([P, S, ROWS], BF16, name="routed%d" % a, align_bytes=64, offset=at)
+            src = picked[a, e * C][:] if a == PASSES - 1 else picked[a, 0][:, :, e * C : (e + 1) * C]
+            interleave(nc.scalar.copy, routed[a][:, e * C : (e + 1) * C, :], src)
+
+        def round_shared(a, c, copy):
             if a == 1:
-                grouped_s[a, c] = reuse.tile([P, COLS, PACK], BF16, name="grouped_s1%d" % c, align_bytes=64, offset=c * 4096)
+                shared[a, c] = reuse.tile([P, COLS, ROWS], BF16, name="shared1%d" % c, align_bytes=64, offset=c * SHARED_BYTES)
             else:
-                grouped_s[a, c] = ring.tile([P, COLS, PACK], BF16, name="grouped_s", bufs=3, align_bytes=64)
-            src = whole[a][:, :, c * COLS : (c + 1) * COLS] if MODES[a] == "P" else dense[a, c][:]
-            interleave(grouped_s[a, c][:], src)
+                shared[a, c] = ring.tile([P, COLS, ROWS], BF16, name="shared", bufs=2 * CHUNKS, align_bytes=64)
+            interleave(copy, shared[a, c][:], first[:, :, c * COLS : (c + 1) * COLS] if a == 0 else dense[a, c][:])
 
-        def multiply(acc, e, a, codes, plane):
-            m = e * PASSES + a
+        def multiply(acc, expert, a, codes, scales):
+            m = expert * PASSES + a
             nc.tensor.matmul_mx(
                 acc[:],
                 lhsT=w_codes[:, m, :].bitcast(E2M1X4),
-                lhsT_scale=w_plane[:, m, :],
+                lhsT_scale=w_bytes[:, m, :],
                 rhs=codes.bitcast(E5M2X4),
-                rhs_scale=plane,
+                rhs_scale=scales,
                 start=(a == 0),
                 stop=(a == PASSES - 1),
             )
 
-        def quantise_routed(a, lo, hi):
-            codes = ring.tile([P, hi - lo], U32, name="codes_r", bufs=2, align_bytes=64)
-            plane = ring.tile([P, hi - lo], U8, name="plane_r", bufs=2, align_bytes=64)
-            nc.vector.quantize_mx(codes[:].bitcast(E5M2X4), plane[:], grouped_r[a][:, lo:hi, :].rearrange("p s t -> p (s t)"))
-            for x in range(lo, hi, C):
+        def product_routed(a, lo, hi):
+            codes = ring.tile([P, hi - lo], U32, name="codes_routed", bufs=2, align_bytes=64)
+            scales = ring.tile([P, hi - lo], U8, name="scales_routed", bufs=2, align_bytes=64)
+            nc.vector.quantize_mx(codes[:].bitcast(E5M2X4), scales[:], routed[a][:, lo:hi, :].rearrange("p s d -> p (s d)"))
+            for e in range(lo // C, hi // C):
                 if a == 0:
-                    acc_r[x // C] = psum.tile([P, COLS], F32, name="acc_r", tag="back", bufs=2)
-                multiply(acc_r[x // C], x // C, a, codes[:, x - lo : x - lo + C], plane[:, x - lo : x - lo + C])
+                    acc_routed[e] = psum.tile([P, C], F32, name="acc_routed", tag="back", bufs=E)
+                cols = slice(e * C - lo, (e + 1) * C - lo)
+                multiply(acc_routed[e], e, a, codes[:, cols], scales[:, cols])
 
-        def quantise_shared(a, c):
-            codes = ring.tile([P, COLS], U32, name="codes_s", bufs=5, align_bytes=64)
+        def product_shared(a, c):
+            codes = ring.tile([P, COLS], U32, name="codes_shared", bufs=5, align_bytes=64)
             if a == 0:
-                plane = reuse.tile([P, COLS], U8, name="plane_first%d" % c, align_bytes=64, offset=12288 + c * COLS)
+                scales = reuse.tile([P, COLS], U8, name="scales_first%d" % c, align_bytes=64, offset=SCALES_AT + c * COLS)
             else:
-                plane = ring.tile([P, COLS], U8, name="plane_s", bufs=5, align_bytes=64)
-            nc.vector.quantize_mx(codes[:].bitcast(E5M2X4), plane[:], grouped_s[a, c][:].rearrange("p s t -> p (s t)"))
-            multiply(acc_s[c], E, a, codes[:], plane[:])
-
-        sums = {}
+                scales = ring.tile([P, COLS], U8, name="scales_shared", bufs=5, align_bytes=64)
+            nc.vector.quantize_mx(codes[:].bitcast(E5M2X4), scales[:], shared[a, c][:].rearrange("p t d -> p (t d)"))
+            if a == 0:
+                acc_shared[c] = psum.tile([P, COLS], F32, name="acc_shared", tag="turned", bufs=AHEAD)
+            multiply(acc_shared[c], E, a, codes[:], scales[:])
 
         def fetch(e):
             sums[e] = keep.tile([P, C], F32, name="sums%d" % e)
-            nc.scalar.copy(sums[e][:], acc_r[e][:])
+            nc.scalar.copy(sums[e][:], acc_routed[e][:])
 
         def scatter(e):
-            nc.vector.tensor_copy(routed_out[:].indirect(offsets[:, e * C // 16 : (e + 1) * C // 16]), sums[e][:])
+            nc.vector.tensor_copy(result[:].indirect(offsets[:, e * C // PER_COL : (e + 1) * C // PER_COL]), sums[e][:])
 
         def finish(c):
             cols = slice(c * COLS, (c + 1) * COLS)
-            total = keep.tile([P, COLS], F32, name="total%d" % c)
-            nc.vector.tensor_tensor(total[:], routed_out[:, cols], acc_s[c][:], ADD)
-            nc.sync.dma_start(out[:, cols], total[:])
+            nc.vector.tensor_tensor(result[:, cols], result[:, cols], acc_shared[c][:], ADD)
+            nc.sync.dma_start(out[:, cols], result[:, cols])
 
-        gather(0, 0, 0, 1024)
-        gather(0, 1, 0, 1024)
-        round_shared(0, 0)
-        round_shared(0, 1)
-        gather(0, 2, 0, 1024)
-        gather(0, 3, 0, 1024)
-        gather(1, 0, 0, 1024)
-        gather(1, 2, 0, 1024)
-        round_shared(0, 2)
-        round_routed(0, 0, 1024)
-        gather(2, 0, 0, 512)
-        quantise_shared(0, 1)
-        round_shared(1, 0)
-        gather(1, 1, 0, 1024)
-        gather(1, 3, 0, 1024)
-        round_routed(1, 0, 512)
-        gather(2, 2, 512, 1024)
-        gather(2, 2, 0, 512)
-        gather(2, 3, 0, 512)
-        gather(2, 1, 0, 512)
-        round_routed(1, 512, 1024)
-        quantise_shared(0, 2)
-        round_routed(2, 0, 512)
-        gather(2, 3, 512, 1024)
-        gather(2, 0, 512, 1024)
-        gather(2, 1, 512, 1024)
-        round_shared(1, 2)
-        quantise_routed(0, 0, 1024)
-        quantise_routed(1, 0, 1024)
-        round_shared(1, 1)
-        quantise_routed(2, 0, 512)
-        quantise_shared(1, 1)
-        round_routed(2, 512, 1024)
+        for d in range(ROWS):
+            gather(0, d, 0, S)
+        for c in range(CHUNKS):
+            round_shared(0, c, nc.scalar.copy)
+        gate_first_pass()
+        for d in range(ROWS):
+            gather(1, d, 0, S)
+        for d in range(ROWS):
+            for e in range(E):
+                gather(last, d, e * C, (e + 1) * C)
+        for c in range(CHUNKS):
+            product_shared(0, c)
+        product_routed(0, 0, S)
+        for e in range(E):
+            round_routed(1, e)
+        product_routed(1, 0, S)
+        for c in range(CHUNKS - 1):
+            for a in (1, last):
+                round_shared(a, c, nc.scalar.copy)
+                product_shared(a, c)
+        round_routed(last, 0)
+        product_routed(last, 0, C)
         fetch(0)
-        quantise_shared(1, 2)
-        quantise_shared(0, 0)
-        quantise_routed(2, 512, 1024)
+        round_shared(1, CHUNKS - 1, nc.vector.tensor_copy)
+        product_shared(1, CHUNKS - 1)
+        round_routed(last, 1)
+        product_routed(last, C, S)
         scatter(0)
-        round_shared(2, 2)
-        round_shared(2, 1)
         fetch(1)
-        quantise_shared(2, 1)
+        round_shared(last, CHUNKS - 1, nc.scalar.copy)
         scatter(1)
-        quantise_shared(1, 0)
-        quantise_shared(2, 2)
-        round_shared(2, 0)
-        quantise_shared(2, 0)
-        finish(2)
-        finish(1)
-        finish(0)
+        product_shared(last, CHUNKS - 1)
+        for c in range(CHUNKS):
+            finish(c)

from contextlib import ExitStack

import concourse.mybir as mybir
from concourse.masks import make_identity

K, T, E, C, N = 128, 1536, 2, 512, 1536
S = E * C
P = 128
ROWS = 4
PASSES = N // (P * ROWS)
COLS = 512
CHUNKS = T // COLS
BLOCKS = S // P
PER_COL = 16
AHEAD = 6
SCALE_ROWS = 4

SHARED_BYTES = COLS * ROWS * 2
SCALES_AT = CHUNKS * SHARED_BYTES
ROUTED_AT = SCALES_AT + CHUNKS * COLS
ROUTED_BYTES = S * ROWS * 2

F32 = mybir.dt.float32
BF16 = mybir.dt.bfloat16
I32 = mybir.dt.int32
U32 = mybir.dt.uint32
U16 = mybir.dt.uint16
U8 = mybir.dt.uint8
E5M2X4 = mybir.dt.float8_e5m2_x4
E2M1X4 = mybir.dt.float4_e2m1fn_x4
MULT = mybir.AluOpType.mult
ADD = mybir.AluOpType.add
COPY = mybir.ActivationFunctionType.Copy

FLOPS = 2 * N * K * (S + T)
BYTES = 4 * N * T + (E + 1) * N * K // 2 + (E + 1) * N * K // 32 + 4 * S + 2 * P * S // PER_COL + 4 * K * T


def tile_moe_bds_lin_none_kernel(tc, dyT, w_words, w_scales, gate, offs, out):
    nc = tc.nc
    with ExitStack() as ctx:
        keep = ctx.enter_context(tc.tile_pool(name="keep", bufs=1))
        ring = ctx.enter_context(tc.tile_pool(name="ring", bufs=2))
        reuse = ctx.enter_context(tc.tile_pool(name="reuse", bufs=1))
        front = ctx.enter_context(tc.tile_pool(name="front", bufs=1))
        psum = ctx.enter_context(tc.psum_pool(name="psum", bufs=1))

        offsets = keep.tile([P, S // PER_COL], U16, name="offsets")
        nc.sync.dma_start(offsets[:], offs)

        dy = [dyT[a * P * ROWS : (a + 1) * P * ROWS, :].rearrange("(p d) t -> p d t", d=ROWS) for a in range(PASSES)]

        w_codes = keep.tile([P, (E + 1) * PASSES, 2 * K], U8, name="w_codes", align_bytes=64)
        w_bytes = keep.tile([P, (E + 1) * PASSES, K], U8, name="w_bytes", align_bytes=64)
        result = keep.tile([P, T], F32, name="result")
        ident = keep.tile([P, P], F32, name="ident")
        gate_rows = keep.tile([P, P], F32, name="gate_rows")
        gate_cols = keep.tile([P, BLOCKS], F32, name="gate_cols")
        gate_all = keep.tile([P, S], F32, name="gate_all")

        nc.vector.memset(w_bytes[:].rearrange("p m k -> p (m k)").bitcast(I32), 0)
        nc.vector.memset(result[:], 0.0)
        make_identity(nc, ident[:])

        first = front.tile([P, ROWS, T], F32, name="first", offset=0)
        window = {}
        dense = {}

        def load_first(d):
            nc.sync.dma_start(first[:, d : d + 1, :], dy[0][:, d : d + 1, :])

        def load_window(a, d):
            window[a, d] = ring.tile([P, T], F32, name="window", bufs=(PASSES - 1) * ROWS)
            nc.sync.dma_start(window[a, d][:], dy[a][:, d, :])

        def load_dense(a, c):
            if a == PASSES - 1:
                dense[a, c] = front.tile([P, ROWS, COLS], F32, name="late%d" % c, offset=c * ROWS * COLS * 4)
            else:
                dense[a, c] = ring.tile([P, ROWS, COLS], F32, name="dense", bufs=CHUNKS)
            nc.sync.dma_start(dense[a, c][:], dy[a][:, :, c * COLS : (c + 1) * COLS])

        def load_gate_rows():
            nc.sync.dma_start(gate_rows[:], gate[0 : P // BLOCKS, :].rearrange("r (b s) -> (r b) s", s=P))

        def load_gate_all():
            nc.sync.dma_start(gate_all[:], gate[0:P, :])

        def load_weight_words():
            nc.sync.dma_start(w_codes[:].bitcast(I32), w_words.rearrange("e a p b -> p (e a) b").bitcast(I32))

        def load_weight_scales():
            by_row = w_scales.rearrange("e a (q r) k -> r q (e a) k", r=SCALE_ROWS)
            for r in range(SCALE_ROWS):
                nc.sync.dma_start(w_bytes[r:P:32].bitcast(I32), by_row[r].bitcast(I32))

        last = PASSES - 1
        load_first(0)
        load_gate_rows()
        for d in range(1, ROWS):
            load_first(d)
        load_gate_all()
        for d in range(ROWS):
            load_window(1, d)
        load_weight_words()
        load_window(last, 0)
        load_weight_scales()
        for d in range(1, ROWS - 1):
            load_window(last, d)
        for c in range(CHUNKS - 1):
            load_dense(1, c)
            load_dense(last, c)
        load_window(last, ROWS - 1)
        load_dense(1, CHUNKS - 1)
        load_dense(last, CHUNKS - 1)

        gate_turned = psum.tile([P, ROWS, P], F32, name="turned", bufs=AHEAD)
        nc.tensor.transpose(gate_turned[:, 0, :], gate_rows[:], ident[:])
        nc.scalar.activation(gate_cols[:], gate_turned[:, 0, 0:BLOCKS], COPY)

        stage = reuse.tile([P, ROWS * S + BLOCKS * 2 * P], F32, name="stage", offset=0)
        picked = {(0, 0): stage[:, 0 : ROWS * S].rearrange("p (d s) -> p d s", d=ROWS)}
        gated = stage[:, ROWS * S :].rearrange("p (b u w) -> p b u w", b=BLOCKS, u=2)
        routed = {}
        shared = {}
        acc_routed = {}
        acc_shared = {}
        sums = {}

        def interleave(copy, dst, src):
            copy(dst.rearrange("p (c i) d -> p c d i", i=2), src.rearrange("p d (c i) -> p c d i", i=2))

        def gather(a, d, lo, hi):
            if (a, lo) not in picked:
                picked[a, lo] = ring.tile([P, ROWS, hi - lo], F32, name="picked%d_%d" % (a, lo), bufs=1)
            slots = offsets[:, lo // PER_COL : hi // PER_COL]
            if a == 0:
                nc.vector.tensor_copy(picked[a, lo][:, d, :], first[:, d, :].indirect(slots))
            else:
                nc.vector.tensor_tensor(picked[a, lo][:, d, :], window[a, d][:].indirect(slots), gate_all[:, lo:hi], MULT)

        def gate_first_pass():
            routed[0] = keep.tile([P, S, ROWS], BF16, name="routed0", align_bytes=64)
            words = routed[0][:].rearrange("p s d -> p (s d)").bitcast(F32)
            turned = {}
            back = {}

            def turn(b):
                turned[b] = psum.tile([P, ROWS, P], F32, name="turned", bufs=AHEAD)
                for d in range(ROWS):
                    nc.tensor.transpose(turned[b][:, d, :], picked[0, 0][:, d, b * P : (b + 1) * P], ident[:])

            for b in range(AHEAD):
                turn(b)
            for b in range(BLOCKS):
                pair, h = divmod(b, 2)
                nc.scalar.activation(
                    gated[:, b, :, :].bitcast(BF16).rearrange("s u (p e) -> s u p e", e=2),
                    turned[b][:].rearrange("s (u e) p -> s u p e", e=2),
                    COPY,
                    scale=gate_cols[:, b : b + 1],
                )
                if b + AHEAD < BLOCKS:
                    turn(b + AHEAD)
                if h == 0:
                    back[pair] = psum.tile([P, 2, 2, P], F32, name="back", bufs=E)
                for u in range(2):
                    nc.tensor.transpose(back[pair][:, h, u, :], gated[:, b, u, :], ident[:])
                if h == 1:
                    nc.scalar.copy(
                        words[:, pair * 4 * P : (pair + 1) * 4 * P].rearrange("p (h s u) -> p h s u", h=2, u=2),
                        back[pair][:].rearrange("p h u s -> p h s u"),
                    )

        def round_routed(a, e):
            if a not in routed:
                at = ROUTED_AT + (a - 1) * ROUTED_BYTES
                routed[a] = reuse.tile([P, S, ROWS], BF16, name="routed%d" % a, align_bytes=64, offset=at)
            src = picked[a, e * C][:] if a == PASSES - 1 else picked[a, 0][:, :, e * C : (e + 1) * C]
            interleave(nc.scalar.copy, routed[a][:, e * C : (e + 1) * C, :], src)

        def round_shared(a, c, copy):
            if a == 1:
                shared[a, c] = reuse.tile([P, COLS, ROWS], BF16, name="shared1%d" % c, align_bytes=64, offset=c * SHARED_BYTES)
            else:
                shared[a, c] = ring.tile([P, COLS, ROWS], BF16, name="shared", bufs=2 * CHUNKS, align_bytes=64)
            interleave(copy, shared[a, c][:], first[:, :, c * COLS : (c + 1) * COLS] if a == 0 else dense[a, c][:])

        def multiply(acc, expert, a, codes, scales):
            m = expert * PASSES + a
            nc.tensor.matmul_mx(
                acc[:],
                lhsT=w_codes[:, m, :].bitcast(E2M1X4),
                lhsT_scale=w_bytes[:, m, :],
                rhs=codes.bitcast(E5M2X4),
                rhs_scale=scales,
                start=(a == 0),
                stop=(a == PASSES - 1),
            )

        def product_routed(a, lo, hi):
            codes = ring.tile([P, hi - lo], U32, name="codes_routed", bufs=2, align_bytes=64)
            scales = ring.tile([P, hi - lo], U8, name="scales_routed", bufs=2, align_bytes=64)
            nc.vector.quantize_mx(codes[:].bitcast(E5M2X4), scales[:], routed[a][:, lo:hi, :].rearrange("p s d -> p (s d)"))
            for e in range(lo // C, hi // C):
                if a == 0:
                    acc_routed[e] = psum.tile([P, C], F32, name="acc_routed", tag="back", bufs=E)
                cols = slice(e * C - lo, (e + 1) * C - lo)
                multiply(acc_routed[e], e, a, codes[:, cols], scales[:, cols])

        def product_shared(a, c):
            codes = ring.tile([P, COLS], U32, name="codes_shared", bufs=5, align_bytes=64)
            if a == 0:
                scales = reuse.tile([P, COLS], U8, name="scales_first%d" % c, align_bytes=64, offset=SCALES_AT + c * COLS)
            else:
                scales = ring.tile([P, COLS], U8, name="scales_shared", bufs=5, align_bytes=64)
            nc.vector.quantize_mx(codes[:].bitcast(E5M2X4), scales[:], shared[a, c][:].rearrange("p t d -> p (t d)"))
            if a == 0:
                acc_shared[c] = psum.tile([P, COLS], F32, name="acc_shared", tag="turned", bufs=AHEAD)
            multiply(acc_shared[c], E, a, codes[:], scales[:])

        def fetch(e):
            sums[e] = keep.tile([P, C], F32, name="sums%d" % e)
            nc.scalar.copy(sums[e][:], acc_routed[e][:])

        def scatter(e):
            nc.vector.tensor_copy(result[:].indirect(offsets[:, e * C // PER_COL : (e + 1) * C // PER_COL]), sums[e][:])

        def finish(c):
            cols = slice(c * COLS, (c + 1) * COLS)
            nc.vector.tensor_tensor(result[:, cols], result[:, cols], acc_shared[c][:], ADD)
            nc.sync.dma_start(out[:, cols], result[:, cols])

        for d in range(ROWS):
            gather(0, d, 0, S)
        for c in range(CHUNKS):
            round_shared(0, c, nc.scalar.copy)
        gate_first_pass()
        for d in range(ROWS):
            gather(1, d, 0, S)
        for d in range(ROWS):
            for e in range(E):
                gather(last, d, e * C, (e + 1) * C)
        for c in range(CHUNKS):
            product_shared(0, c)
        product_routed(0, 0, S)
        for e in range(E):
            round_routed(1, e)
        product_routed(1, 0, S)
        for c in range(CHUNKS - 1):
            for a in (1, last):
                round_shared(a, c, nc.scalar.copy)
                product_shared(a, c)
        round_routed(last, 0)
        product_routed(last, 0, C)
        fetch(0)
        round_shared(1, CHUNKS - 1, nc.vector.tensor_copy)
        product_shared(1, CHUNKS - 1)
        round_routed(last, 1)
        product_routed(last, C, S)
        scatter(0)
        fetch(1)
        round_shared(last, CHUNKS - 1, nc.scalar.copy)
        scatter(1)
        product_shared(last, CHUNKS - 1)
        for c in range(CHUNKS):
            finish(c)
